import numpy as np
import ml_dtypes

BF16 = ml_dtypes.bfloat16


def bf(x):
    return np.asarray(x, np.float32).astype(BF16)


def f32(x):
    return np.asarray(x, np.float32)


def f64(x):
    return np.asarray(x).astype(np.float64)


def striped(idx):
    return np.concatenate([l.reshape(-1, 16).T for l in idx])


def rows(idx, k):
    return np.tile(np.repeat(idx, 16, axis=0), (k // (16 * 8), 1))


def look(tab, idx):
    return np.take_along_axis(f64(tab), rows(idx, len(tab)), axis=1)


K, S, V, N = 512, 2048, 1024, 1024


def setup_inputs():
    return {"tab": f32(np.random.standard_normal((2, K, S))), "x0": f32(np.random.standard_normal((K, V))), "offs": striped(np.random.randint(0, S, (8, N)))}


def reference(tab, x0, offs):
    idx = np.stack([g.T.reshape(-1) for g in np.split(offs, 8)])
    x = f64(x0) * look(tab[0], idx) + look(tab[1], idx)
    return x

@@ -1,0 +1,36 @@
+import concourse.mybir as mybir
+
+P = 128
+F32 = mybir.dt.float32
+U16 = mybir.dt.uint16
+MULT = mybir.AluOpType.mult
+ADD = mybir.AluOpType.add
+
+
+def tile_lookup_film_mul_out_kernel(tc, tab, x0, offs, out):
+    nc = tc.nc
+    rows, ids = tab.shape[1], tab.shape[2]
+    entries = x0.shape[1]
+    blocks = rows // P
+
+    with tc.tile_pool(name="held", bufs=1) as held:
+        offsets = held.tile([P, offs.shape[1]], U16, name="offsets")
+        nc.sync.dma_start(offsets[:], offs)
+
+        gains, shifts, features = [], [], []
+        for b in range(blocks):
+            block = slice(b * P, (b + 1) * P)
+            gains.append(held.tile([P, ids], F32, name=f"gains{b}"))
+            features.append(held.tile([P, entries], F32, name=f"features{b}"))
+            shifts.append(held.tile([P, ids], F32, name=f"shifts{b}"))
+            nc.sync.dma_start(gains[b][:], tab[0, block, :])
+            nc.sync.dma_start(features[b][:], x0[block, :])
+            nc.sync.dma_start(shifts[b][:], tab[1, block, :])
+
+        for b in range(blocks):
+            block = slice(b * P, (b + 1) * P)
+            scaled = held.tile([P, entries], F32, name=f"scaled{b}")
+            result = held.tile([P, entries], F32, name=f"result{b}")
+            nc.vector.tensor_tensor(scaled[:], gains[b][:].indirect(offsets[:]), features[b][:], MULT)
+            nc.vector.tensor_tensor(result[:], shifts[b][:].indirect(offsets[:]), scaled[:], ADD)
+            nc.sync.dma_start(out[block, :], result[:])

@@ -1,6 +1,7 @@
 import concourse.mybir as mybir
 
 P = 128
+GROUP = 16
 F32 = mybir.dt.float32
 U16 = mybir.dt.uint16
 MULT = mybir.AluOpType.mult
@@ -15,7 +16,6 @@ def tile_lookup_film_mul_out_kernel(tc, tab, x0, offs, out):
 
     with tc.tile_pool(name="held", bufs=1) as held:
         offsets = held.tile([P, offs.shape[1]], U16, name="offsets")
-        nc.sync.dma_start(offsets[:], offs)
 
         gains, shifts, features = [], [], []
         for b in range(blocks):
@@ -24,6 +24,8 @@ def tile_lookup_film_mul_out_kernel(tc, tab, x0, offs, out):
             features.append(held.tile([P, entries], F32, name=f"features{b}"))
             shifts.append(held.tile([P, ids], F32, name=f"shifts{b}"))
             nc.sync.dma_start(gains[b][:], tab[0, block, :])
+            if b == 0:
+                nc.sync.dma_start(offsets[:], offs)
             nc.sync.dma_start(features[b][:], x0[block, :])
             nc.sync.dma_start(shifts[b][:], tab[1, block, :])
 
@@ -32,5 +34,10 @@ def tile_lookup_film_mul_out_kernel(tc, tab, x0, offs, out):
             scaled = held.tile([P, entries], F32, name=f"scaled{b}")
             result = held.tile([P, entries], F32, name=f"result{b}")
             nc.vector.tensor_tensor(scaled[:], gains[b][:].indirect(offsets[:]), features[b][:], MULT)
-            nc.vector.tensor_tensor(result[:], shifts[b][:].indirect(offsets[:]), scaled[:], ADD)
-            nc.sync.dma_start(out[block, :], result[:])
+            pieces = 2 if b == blocks - 1 else 1
+            width = entries // pieces
+            for k in range(pieces):
+                cols = slice(k * width, (k + 1) * width)
+                piece_offsets = offsets[:, k * width // GROUP : (k + 1) * width // GROUP]
+                nc.vector.tensor_tensor(result[:, cols], shifts[b][:].indirect(piece_offsets), scaled[:, cols], ADD)
+                nc.sync.dma_start(out[block, cols], result[:, cols])

@@ -14,8 +14,16 @@ def tile_lookup_film_mul_out_kernel(tc, tab, x0, offs, out):
     entries = x0.shape[1]
     blocks = rows // P
 
+    def pieces(b):
+        count = 2 if b == blocks - 1 else 1
+        width = entries // count
+        return [slice(k * width, (k + 1) * width) for k in range(count)]
+
     with tc.tile_pool(name="held", bufs=1) as held:
         offsets = held.tile([P, offs.shape[1]], U16, name="offsets")
+
+        def offsets_of(cols):
+            return offsets[:, cols.start // GROUP : cols.stop // GROUP]
 
         gains, shifts, features = [], [], []
         for b in range(blocks):
@@ -26,18 +34,18 @@ def tile_lookup_film_mul_out_kernel(tc, tab, x0, offs, out):
             nc.sync.dma_start(gains[b][:], tab[0, block, :])
             if b == 0:
                 nc.sync.dma_start(offsets[:], offs)
-            nc.sync.dma_start(features[b][:], x0[block, :])
+            for cols in pieces(b):
+                nc.sync.dma_start(features[b][:, cols], x0[block, cols])
             nc.sync.dma_start(shifts[b][:], tab[1, block, :])
 
         for b in range(blocks):
             block = slice(b * P, (b + 1) * P)
             scaled = held.tile([P, entries], F32, name=f"scaled{b}")
             result = held.tile([P, entries], F32, name=f"result{b}")
-            nc.vector.tensor_tensor(scaled[:], gains[b][:].indirect(offsets[:]), features[b][:], MULT)
-            pieces = 2 if b == blocks - 1 else 1
-            width = entries // pieces
-            for k in range(pieces):
-                cols = slice(k * width, (k + 1) * width)
-                piece_offsets = offsets[:, k * width // GROUP : (k + 1) * width // GROUP]
-                nc.vector.tensor_tensor(result[:, cols], shifts[b][:].indirect(piece_offsets), scaled[:, cols], ADD)
+            for cols in pieces(b):
+                nc.vector.tensor_tensor(
+                    scaled[:, cols], gains[b][:].indirect(offsets_of(cols)), features[b][:, cols], MULT
+                )
+            for cols in pieces(b):
+                nc.vector.tensor_tensor(result[:, cols], shifts[b][:].indirect(offsets_of(cols)), scaled[:, cols], ADD)
                 nc.sync.dma_start(out[block, cols], result[:, cols])

import concourse.mybir as mybir

P = 128
GROUP = 16
F32 = mybir.dt.float32
U16 = mybir.dt.uint16
MULT = mybir.AluOpType.mult
ADD = mybir.AluOpType.add


def tile_lookup_film_mul_out_kernel(tc, tab, x0, offs, out):
    nc = tc.nc
    rows, ids = tab.shape[1], tab.shape[2]
    entries = x0.shape[1]
    blocks = rows // P

    def pieces(b):
        count = 2 if b == blocks - 1 else 1
        width = entries // count
        return [slice(k * width, (k + 1) * width) for k in range(count)]

    with tc.tile_pool(name="held", bufs=1) as held:
        offsets = held.tile([P, offs.shape[1]], U16, name="offsets")

        def offsets_of(cols):
            return offsets[:, cols.start // GROUP : cols.stop // GROUP]

        gains, shifts, features = [], [], []
        for b in range(blocks):
            block = slice(b * P, (b + 1) * P)
            gains.append(held.tile([P, ids], F32, name=f"gains{b}"))
            features.append(held.tile([P, entries], F32, name=f"features{b}"))
            shifts.append(held.tile([P, ids], F32, name=f"shifts{b}"))
            nc.sync.dma_start(gains[b][:], tab[0, block, :])
            if b == 0:
                nc.sync.dma_start(offsets[:], offs)
            for cols in pieces(b):
                nc.sync.dma_start(features[b][:, cols], x0[block, cols])
            nc.sync.dma_start(shifts[b][:], tab[1, block, :])

        for b in range(blocks):
            block = slice(b * P, (b + 1) * P)
            scaled = held.tile([P, entries], F32, name=f"scaled{b}")
            result = held.tile([P, entries], F32, name=f"result{b}")
            for cols in pieces(b):
                nc.vector.tensor_tensor(
                    scaled[:, cols], gains[b][:].indirect(offsets_of(cols)), features[b][:, cols], MULT
                )
            for cols in pieces(b):
                nc.vector.tensor_tensor(result[:, cols], shifts[b][:].indirect(offsets_of(cols)), scaled[:, cols], ADD)
                nc.sync.dma_start(out[block, cols], result[:, cols])
